import numpy as np
import ml_dtypes


def mxq(x, axis, fmt="e4m3"):
    dtype, down = {"e4m3": (ml_dtypes.float8_e4m3fn, 7), "e5m2": (ml_dtypes.float8_e5m2, 14)}[fmt]
    v = np.moveaxis(np.asarray(x, np.float32).astype(ml_dtypes.bfloat16).astype(np.float64), axis, -1)
    blocks = v.reshape(v.shape[:-1] + (-1, 32))
    amax = np.abs(blocks).max(-1, keepdims=True)
    byte = np.maximum(np.where(amax > 0, np.frexp(amax)[1] - 1 + 127, 0) - down, 1)
    scale = np.exp2(byte - 127.0)
    codes = (blocks / scale).astype(np.float32).astype(dtype).astype(np.float64)
    return np.moveaxis((codes * scale).reshape(v.shape), -1, axis)


WIDE = False


def mx_kscale(k):
    if not WIDE:
        return np.ones(k)
    levels = np.array([30, -30])
    if k % 512:
        return np.exp2(np.random.permutation(np.resize(levels, k // 32))).repeat(32)
    a = np.empty((k // 512, 16))
    for p in range(k // 512):
        a[p, :8] = np.random.permutation(np.resize(levels, 8))
        for g in range(8):
            far = levels[np.abs(levels - a[p, g]) >= 10]
            a[p, g + 8] = far[np.random.randint(len(far))]
    return np.exp2(a.ravel()).repeat(32)


def f64(x):
    return np.asarray(x).astype(np.float64)


def striped(idx):
    return np.tile(np.asarray(idx).reshape(-1, 16).T, (8, 1)).astype(np.uint16)


def unstriped(offs):
    return offs[:16].T.reshape(-1).astype(np.int64)


E2M1 = np.array([0.0, 0.5, 1.0, 1.5, 2.0, 3.0, 4.0, 6.0, -0.0, -0.5, -1.0, -1.5, -2.0, -3.0, -4.0, -6.0])


def pack_weight(w, fmt):
    k, n = w.shape
    w = f64(np.asarray(w, np.float32).astype(ml_dtypes.bfloat16)).reshape(k // 32, 32, n)
    amax = np.abs(w).max(1)
    if fmt in ("e4m3", "e5m2"):
        byte = np.frexp(amax)[1] - 1 + 127 - (7 if fmt == "e4m3" else 14)
    else:
        mant, ex = np.frexp(amax / 6.0)
        byte = np.where(mant > 0.5, ex, ex - 1) + 127
    byte = np.clip(np.where(amax > 0, byte, 1), 1, 254)
    scaled = (w * np.exp2(127.0 - byte)[:, None, :]).reshape(k, n).astype(np.float32)
    by_word = np.ascontiguousarray(scaled.reshape(k // 512, 128, 4, n).transpose(0, 1, 3, 2))
    if fmt in ("e4m3", "e5m2"):
        words = by_word.astype(ml_dtypes.float8_e4m3fn if fmt == "e4m3" else ml_dtypes.float8_e5m2).view(np.uint8)
    else:
        c = by_word.astype(ml_dtypes.float4_e2m1fn).view(np.uint8) & 0xF
        words = (c[..., 0::2] | (c[..., 1::2] << 4)).reshape(k // 512, 128, 2 * n)
    return np.ascontiguousarray(words), np.ascontiguousarray(byte.astype(np.uint8).reshape(k // 512, 16, n))


def unpack_weight(words, scales, fmt):
    g, _, n = scales.shape
    words = np.ascontiguousarray(words).reshape(g, 128, n, -1)
    if fmt in ("e4m3", "e5m2"):
        vals = words.view(ml_dtypes.float8_e4m3fn if fmt == "e4m3" else ml_dtypes.float8_e5m2).astype(np.float64)
    else:
        nib = np.empty((g, 128, n, 4), np.uint8)
        nib[..., 0::2] = words & 0xF
        nib[..., 1::2] = words >> 4
        vals = E2M1[nib]
    vals = vals * np.repeat(np.exp2(scales.astype(np.float64) - 127.0), 8, axis=1)[..., None]
    return vals.transpose(0, 1, 3, 2).reshape(g * 512, n)


K, T, J, I, R, V = 512, 512, 256, 256, 512, 512


def setup_inputs():
    n = np.random.standard_normal
    idx = np.random.permutation(T)[:J]
    idx2 = np.random.permutation(V)[:J]
    idx3 = np.random.permutation(T)[:I]
    fk = mx_kscale(K)
    fr = mx_kscale(R)
    xtp = pack_weight(n((K, T)) / fk[:, None], "e2m1")
    wap = pack_weight(n((K, R)) * 0.5 / np.sqrt(K) * fk[:, None] * fr, "e2m1")
    wbp = pack_weight(n((K, R)) * 1 / np.sqrt(K) * fk[:, None] / fr, "e5m2")
    return {
        "xt_words": xtp[0],
        "xt_scales": xtp[1],
        "wa_words": wap[0],
        "wa_scales": wap[1],
        "tb": (n((R, V)) * 0.5 * fr[:, None]).astype(np.float32),
        "wb_words": wbp[0],
        "wb_scales": wbp[1],
        "bi": (np.random.uniform(-15.0, 15.0, (1, I))).astype(np.float32),
        "offs": striped(idx),
        "offs2": striped(idx2),
        "offs3": striped(idx3),
    }


def reference(xt_words, xt_scales, wa_words, wa_scales, tb, wb_words, wb_scales, bi, offs, offs2, offs3):
    idx = unstriped(offs)
    idx2 = unstriped(offs2)
    idx3 = unstriped(offs3)
    xtu = unpack_weight(xt_words, xt_scales, "e2m1")
    wau = unpack_weight(wa_words, wa_scales, "e2m1")
    wbu = unpack_weight(wb_words, wb_scales, "e5m2")
    xtidxg = xtu[:, idx]
    za = wau.T @ xtidxg
    ha = np.maximum(za - f64(tb)[:, idx2], 0.0)
    xtidx3g = xtu[:, idx3]
    zb = wbu.T @ xtidx3g
    hb = np.maximum(zb, 0.0)
    haq = mxq(ha, 0, "e5m2")
    hbq = mxq(hb, 0, "e4m3")
    a0 = haq.T @ hbq
    a = a0 + f64(bi)
    mn = np.mean(a, axis=1, keepdims=True)
    d = a - mn
    y = d / (np.mean(np.abs(d), axis=1, keepdims=True) + 4.0)
    return y

@@ -1,0 +1,192 @@
+from contextlib import ExitStack
+
+import concourse.mybir as mybir
+from concourse.masks import make_identity
+
+K, T, J, I, R, V = 512, 512, 256, 256, 512, 512
+FLOPS = 2 * K * R * (J + I) + 2 * R * J * I
+
+F32 = mybir.dt.float32
+BF16 = mybir.dt.bfloat16
+I32 = mybir.dt.int32
+U32 = mybir.dt.uint32
+U16 = mybir.dt.uint16
+U8 = mybir.dt.uint8
+E2M1 = mybir.dt.float4_e2m1fn_x4
+E5M2 = mybir.dt.float8_e5m2_x4
+E4M3 = mybir.dt.float8_e4m3fn_x4
+ALU = mybir.AluOpType
+ACT = mybir.ActivationFunctionType
+
+P = 128
+PACK = 4
+HALF = 128
+
+
+def tile_list_meet_overtable_plain_spread_kernel(
+    tc, xt_words, xt_scales, wa_words, wa_scales, tb, wb_words, wb_scales, bi, offs, offs2, offs3, out
+):
+    nc = tc.nc
+    with ExitStack() as ctx:
+        sb = ctx.enter_context(tc.tile_pool(name="sb", bufs=1))
+        ps = ctx.enter_context(tc.psum_pool(name="ps", bufs=1))
+
+        def load_scale_rows(queue, plane, scales):
+            for q in range(4):
+                queue.dma_start(out=plane[32 * q : 32 * q + 4, :].bitcast(I32), in_=scales[0, 4 * q : 4 * q + 4, :].bitcast(I32))
+
+        list_j = sb.tile([P, J // 16], U16, name="list_j")
+        list_v = sb.tile([P, J // 16], U16, name="list_v")
+        list_i = sb.tile([P, I // 16], U16, name="list_i")
+        x_w = sb.tile([P, T], U16, name="x_w", align_bytes=64)
+        x_s = sb.tile([P, T], U8, name="x_s", align_bytes=64)
+        wa_raw = sb.tile([P, R // 2], U32, name="wa_raw", align_bytes=64)
+        wb_raw = sb.tile([P, R], U32, name="wb_raw", align_bytes=64)
+        was_raw = sb.tile([P, R // 4], U32, name="was_raw", align_bytes=64)
+        wbs_raw = sb.tile([P, R // 4], U32, name="wbs_raw", align_bytes=64)
+        tb_rows = [sb.tile([P, V], F32, name=f"tb_rows{t}", align_bytes=64) for t in range(PACK)]
+        bi_col = sb.tile([P, 8], F32, name="bi_col")
+        ident = sb.tile([P, P], F32, name="ident")
+
+        nc.vector.memset(x_s[:].bitcast(I32), 0)
+        nc.vector.memset(was_raw[:].bitcast(I32), 0)
+        nc.vector.memset(wbs_raw[:].bitcast(I32), 0)
+
+        tb_view = tb.rearrange("(b t q) v -> t b q v", t=PACK, q=8)
+        for t in range(1, PACK):
+            nc.gpsimd.dma_start(out=tb_rows[t][:], in_=tb_view[t])
+        nc.sync.dma_start(out=x_w[:].bitcast(I32), in_=xt_words[0].bitcast(I32))
+        nc.sync.dma_start(list_j[:], offs)
+        load_scale_rows(nc.scalar, x_s, xt_scales)
+        nc.sync.dma_start(list_v[:], offs2)
+        nc.sync.dma_start(out=tb_rows[0][:], in_=tb_view[0])
+        nc.sync.dma_start(out=wa_raw[:].bitcast(I32), in_=wa_words[0].bitcast(I32))
+        load_scale_rows(nc.scalar, was_raw, wa_scales)
+        nc.sync.dma_start(list_i[:], offs3)
+        nc.sync.dma_start(out=wb_raw[:].bitcast(I32), in_=wb_words[0].rearrange("p n t -> p (n t)").bitcast(I32))
+        load_scale_rows(nc.sync, wbs_raw, wb_scales)
+        with nc.allow_non_contiguous_dma(reason="one bias value to a partition"):
+            nc.sync.dma_start(out=bi_col[:, 0:2], in_=bi.rearrange("o (c p) -> p (o c)", p=P))
+        make_identity(nc, ident[:])
+
+        xa_w = sb.tile([P, J], U16, name="xa_w", align_bytes=64)
+        xa_s = sb.tile([P, J], U8, name="xa_s", align_bytes=64)
+        xb_w = sb.tile([P, I], U16, name="xb_w", align_bytes=64)
+        xb_s = sb.tile([P, I], U8, name="xb_s", align_bytes=64)
+        nc.vector.tensor_copy(xa_w[:], x_w[:].indirect(list_j[:]))
+        nc.vector.tensor_copy(xa_s[:], x_s[:].indirect(list_j[:]))
+
+        def deal(engine_copy, dst, src, run):
+            engine_copy(
+                dst[:].rearrange("p (t b w) -> p t b w", t=PACK, w=run),
+                src[:].rearrange("p (b t w) -> p t b w", t=PACK, w=run),
+            )
+
+        wa_w = sb.tile([P, R // 2], U32, name="wa_w", align_bytes=64)
+        wa_s = sb.tile([P, R // 4], U32, name="wa_s", align_bytes=64)
+        wb_w = sb.tile([P, R], U32, name="wb_w", align_bytes=64)
+        wb_s = sb.tile([P, R // 4], U32, name="wb_s", align_bytes=64)
+        tb_g = [sb.tile([P, J], F32, name=f"tb_g{t}", align_bytes=64) for t in range(PACK)]
+
+        nc.scalar.activation(tb_g[0][:], tb_rows[0][:].indirect(list_v[:]), ACT.Copy)
+        deal(nc.scalar.copy, wa_w, wa_raw, 4)
+        deal(nc.scalar.copy, wa_s, was_raw, 2)
+        nc.scalar.activation(tb_g[1][:], tb_rows[1][:].indirect(list_v[:]), ACT.Copy)
+
+        nc.vector.tensor_copy(xb_w[:], x_w[:].indirect(list_i[:]))
+        nc.vector.tensor_copy(xb_s[:], x_s[:].indirect(list_i[:]))
+
+        za = [ps.tile([P, 2, J], F32, name=f"za{u}") for u in range(2)]
+        for t in range(PACK):
+            nc.tensor.matmul_mx(
+                out=za[t // 2][:, t % 2, :],
+                lhsT=wa_w[:, 64 * t : 64 * (t + 1)].bitcast(E2M1),
+                lhsT_scale=wa_s[:, 32 * t : 32 * (t + 1)].bitcast(U8),
+                rhs=xa_w[:].bitcast(E2M1),
+                rhs_scale=xa_s[:],
+                start=True,
+                stop=True,
+            )
+
+        deal(nc.scalar.copy, wb_w, wb_raw, 8)
+        for t in range(2, PACK):
+            nc.scalar.activation(tb_g[t][:], tb_rows[t][:].indirect(list_v[:]), ACT.Copy)
+        deal(nc.scalar.copy, wb_s, wbs_raw, 2)
+
+        zb = [ps.tile([P, PACK, HALF], F32, name=f"zb{h}", tag=f"zb{h}") for h in range(2)]
+        for h in range(2):
+            cols = slice(HALF * h, HALF * (h + 1))
+            for t in range(PACK):
+                nc.tensor.matmul_mx(
+                    out=zb[h][:, t, :],
+                    lhsT=wb_w[:, P * t : P * (t + 1)].bitcast(E5M2),
+                    lhsT_scale=wb_s[:, 32 * t : 32 * (t + 1)].bitcast(U8),
+                    rhs=xb_w[:, cols].bitcast(E2M1),
+                    rhs_scale=xb_s[:, cols],
+                    start=True,
+                    stop=True,
+                )
+
+        diff = sb.tile([P, PACK, J], BF16, name="diff", align_bytes=64)
+        for t in range(PACK):
+            nc.vector.tensor_tensor(diff[:, t, :], za[t // 2][:, t % 2, :], tb_g[t][:], ALU.subtract)
+
+        hb = [sb.tile([P, HALF, PACK], BF16, name=f"hb{h}", align_bytes=64) for h in range(2)]
+        ha = [sb.tile([P, HALF, PACK], BF16, name=f"ha{h}", align_bytes=64) for h in range(2)]
+        hb_w = sb.tile([P, I], U32, name="hb_w", align_bytes=64)
+        hb_s = sb.tile([P, I], U8, name="hb_s", align_bytes=64)
+        ha_w = [sb.tile([P, HALF], U32, name=f"ha_w{h}", align_bytes=64) for h in range(2)]
+        ha_s = [sb.tile([P, HALF], U8, name=f"ha_s{h}", align_bytes=64) for h in range(2)]
+        for h in range(2):
+            nc.scalar.activation(hb[h][:], zb[h][:].rearrange("p t i -> p i t"), ACT.Relu)
+        bias_ps = ps.tile([P, I], F32, name="bias_ps", tag="zb0")
+        for c in range(2):
+            nc.tensor.transpose(bias_ps[:, P * c : P * (c + 1)], bi_col[:, c : c + 1].to_broadcast([P, P]), ident[:])
+        nbias = sb.tile([P, I], F32, name="nbias", align_bytes=64)
+        nc.scalar.activation(nbias[:], bias_ps[:], ACT.Copy, scale=-1.0 / I)
+
+        def relu_weave(h):
+            nc.vector.tensor_scalar(
+                ha[h][:].rearrange("p (c e) t -> p c t e", e=4),
+                diff[:, :, HALF * h : HALF * (h + 1)].rearrange("p t (c e) -> p c t e", e=4),
+                0.0,
+                None,
+                ALU.max,
+            )
+
+        def quantize(words, scales, src, fmt):
+            nc.vector.quantize_mx(out=words.bitcast(fmt), scales=scales, in_=src[:].rearrange("p c t -> p (c t)"))
+
+        relu_weave(0)
+        quantize(hb_w[:, 0:HALF], hb_s[:, 0:HALF], hb[0], E4M3)
+        relu_weave(1)
+        quantize(ha_w[0][:], ha_s[0][:], ha[0], E5M2)
+        quantize(hb_w[:, HALF:I], hb_s[:, HALF:I], hb[1], E4M3)
+        quantize(ha_w[1][:], ha_s[1][:], ha[1], E5M2)
+
+        for h in range(2):
+            a0 = ps.tile([P, I], F32, name=f"a0_{h}")
+            nc.tensor.matmul_mx(
+                out=a0[:],
+                lhsT=ha_w[h][:].bitcast(E5M2),
+                lhsT_scale=ha_s[h][:],
+                rhs=hb_w[:].bitcast(E4M3),
+                rhs_scale=hb_s[:],
+                start=True,
+                stop=True,
+            )
+            na = sb.tile([P, I], F32, name=f"na{h}", align_bytes=64)
+            nmean = sb.tile([P, 1], F32, name=f"nmean{h}")
+            nc.vector.scalar_tensor_tensor(na[:], a0[:], -1.0 / I, nbias[:], ALU.mult, ALU.add, accum_out=nmean[:])
+            mag = sb.tile([P, I], F32, name=f"mag{h}", align_bytes=64)
+            mag_sum = sb.tile([P, 1], F32, name=f"mag_sum{h}")
+            nc.scalar.activation(mag[:], na[:], ACT.Abs, bias=nmean[:], scale=-float(I), accum_out=mag_sum[:])
+            d = sb.tile([P, I], F32, name=f"d{h}", align_bytes=64)
+            nc.vector.tensor_scalar(d[:], na[:], -float(I), nmean[:], ALU.mult, ALU.add)
+            den = sb.tile([P, 1], F32, name=f"den{h}")
+            nc.vector.tensor_scalar(den[:], mag_sum[:], 1.0 / I, 4.0, ALU.mult, ALU.add)
+            rec = sb.tile([P, 1], F32, name=f"rec{h}")
+            nc.vector.reciprocal(rec[:], den[:])
+            y = sb.tile([P, I], F32, name=f"y{h}", align_bytes=64)
+            nc.vector.tensor_scalar(y[:], d[:], rec[:], None, ALU.mult)
+            nc.sync.dma_start(out=out[P * h : P * (h + 1), :], in_=y[:])

@@ -31,8 +31,8 @@ def tile_list_meet_overtable_plain_spread_kernel(
         sb = ctx.enter_context(tc.tile_pool(name="sb", bufs=1))
         ps = ctx.enter_context(tc.psum_pool(name="ps", bufs=1))
 
-        def load_scale_rows(queue, plane, scales):
-            for q in range(4):
+        def load_scale_rows(queue, plane, scales, quadrants):
+            for q in quadrants:
                 queue.dma_start(out=plane[32 * q : 32 * q + 4, :].bitcast(I32), in_=scales[0, 4 * q : 4 * q + 4, :].bitcast(I32))
 
         list_j = sb.tile([P, J // 16], U16, name="list_j")
@@ -48,23 +48,24 @@ def tile_list_meet_overtable_plain_spread_kernel(
         bi_col = sb.tile([P, 8], F32, name="bi_col")
         ident = sb.tile([P, P], F32, name="ident")
 
+        tb_view = tb.rearrange("(b t q) v -> t b q v", t=PACK, q=8)
         nc.vector.memset(x_s[:].bitcast(I32), 0)
         nc.vector.memset(was_raw[:].bitcast(I32), 0)
         nc.vector.memset(wbs_raw[:].bitcast(I32), 0)
-
-        tb_view = tb.rearrange("(b t q) v -> t b q v", t=PACK, q=8)
-        for t in range(1, PACK):
-            nc.gpsimd.dma_start(out=tb_rows[t][:], in_=tb_view[t])
-        nc.sync.dma_start(out=x_w[:].bitcast(I32), in_=xt_words[0].bitcast(I32))
         nc.sync.dma_start(list_j[:], offs)
-        load_scale_rows(nc.scalar, x_s, xt_scales)
-        nc.sync.dma_start(list_v[:], offs2)
+        nc.scalar.dma_start(out=x_w[:].bitcast(I32), in_=xt_words[0].bitcast(I32))
+        load_scale_rows(nc.sync, x_s, xt_scales, (0, 1))
+        load_scale_rows(nc.scalar, x_s, xt_scales, (2, 3))
         nc.sync.dma_start(out=tb_rows[0][:], in_=tb_view[0])
+        nc.scalar.dma_start(out=tb_rows[1][:], in_=tb_view[1])
         nc.sync.dma_start(out=wa_raw[:].bitcast(I32), in_=wa_words[0].bitcast(I32))
-        load_scale_rows(nc.scalar, was_raw, wa_scales)
+        nc.sync.dma_start(list_v[:], offs2)
+        load_scale_rows(nc.sync, was_raw, wa_scales, range(4))
         nc.sync.dma_start(list_i[:], offs3)
         nc.sync.dma_start(out=wb_raw[:].bitcast(I32), in_=wb_words[0].rearrange("p n t -> p (n t)").bitcast(I32))
-        load_scale_rows(nc.sync, wbs_raw, wb_scales)
+        nc.sync.dma_start(out=tb_rows[2][:], in_=tb_view[2])
+        load_scale_rows(nc.sync, wbs_raw, wb_scales, range(4))
+        nc.sync.dma_start(out=tb_rows[3][:], in_=tb_view[3])
         with nc.allow_non_contiguous_dma(reason="one bias value to a partition"):
             nc.sync.dma_start(out=bi_col[:, 0:2], in_=bi.rearrange("o (c p) -> p (o c)", p=P))
         make_identity(nc, ident[:])
@@ -88,9 +89,9 @@ def tile_list_meet_overtable_plain_spread_kernel(
         wb_s = sb.tile([P, R // 4], U32, name="wb_s", align_bytes=64)
         tb_g = [sb.tile([P, J], F32, name=f"tb_g{t}", align_bytes=64) for t in range(PACK)]
 
-        nc.scalar.activation(tb_g[0][:], tb_rows[0][:].indirect(list_v[:]), ACT.Copy)
         deal(nc.scalar.copy, wa_w, wa_raw, 4)
-        deal(nc.scalar.copy, wa_s, was_raw, 2)
+        deal(nc.vector.tensor_copy, wa_s, was_raw, 2)
+        nc.scalar.activation(tb_g[0][:], tb_rows[0][:].indirect(list_v[:]), ACT.Copy)
         nc.scalar.activation(tb_g[1][:], tb_rows[1][:].indirect(list_v[:]), ACT.Copy)
 
         nc.vector.tensor_copy(xb_w[:], x_w[:].indirect(list_i[:]))
@@ -108,10 +109,20 @@ def tile_list_meet_overtable_plain_spread_kernel(
                 stop=True,
             )
 
-        deal(nc.scalar.copy, wb_w, wb_raw, 8)
-        for t in range(2, PACK):
-            nc.scalar.activation(tb_g[t][:], tb_rows[t][:].indirect(list_v[:]), ACT.Copy)
-        deal(nc.scalar.copy, wb_s, wbs_raw, 2)
+        nc.scalar.activation(tb_g[2][:], tb_rows[2][:].indirect(list_v[:]), ACT.Copy)
+        nc.scalar.activation(tb_g[3][:], tb_rows[3][:].indirect(list_v[:]), ACT.Copy)
+
+        diff = sb.tile([P, PACK, J], BF16, name="diff", align_bytes=64)
+
+        def take_off(t):
+            nc.vector.tensor_tensor(diff[:, t, :], za[t // 2][:, t % 2, :], tb_g[t][:], ALU.subtract)
+
+        take_off(0)
+        take_off(1)
+        deal(nc.gpsimd.tensor_copy, wb_w, wb_raw, 8)
+        deal(nc.gpsimd.tensor_copy, wb_s, wbs_raw, 2)
+        take_off(2)
+        take_off(3)
 
         zb = [ps.tile([P, PACK, HALF], F32, name=f"zb{h}", tag=f"zb{h}") for h in range(2)]
         for h in range(2):
@@ -126,10 +137,6 @@ def tile_list_meet_overtable_plain_spread_kernel(
                     start=True,
                     stop=True,
                 )
-
-        diff = sb.tile([P, PACK, J], BF16, name="diff", align_bytes=64)
-        for t in range(PACK):
-            nc.vector.tensor_tensor(diff[:, t, :], za[t // 2][:, t % 2, :], tb_g[t][:], ALU.subtract)
 
         hb = [sb.tile([P, HALF, PACK], BF16, name=f"hb{h}", align_bytes=64) for h in range(2)]
         ha = [sb.tile([P, HALF, PACK], BF16, name=f"ha{h}", align_bytes=64) for h in range(2)]
@@ -181,12 +188,12 @@ def tile_list_meet_overtable_plain_spread_kernel(
             mag = sb.tile([P, I], F32, name=f"mag{h}", align_bytes=64)
             mag_sum = sb.tile([P, 1], F32, name=f"mag_sum{h}")
             nc.scalar.activation(mag[:], na[:], ACT.Abs, bias=nmean[:], scale=-float(I), accum_out=mag_sum[:])
-            d = sb.tile([P, I], F32, name=f"d{h}", align_bytes=64)
-            nc.vector.tensor_scalar(d[:], na[:], -float(I), nmean[:], ALU.mult, ALU.add)
+            shift = sb.tile([P, 1], F32, name=f"shift{h}")
+            nc.vector.tensor_scalar(shift[:], nmean[:], -1.0 / I, None, ALU.mult)
             den = sb.tile([P, 1], F32, name=f"den{h}")
-            nc.vector.tensor_scalar(den[:], mag_sum[:], 1.0 / I, 4.0, ALU.mult, ALU.add)
+            nc.vector.tensor_scalar(den[:], mag_sum[:], -1.0 / (I * I), -4.0 / I, ALU.mult, ALU.add)
             rec = sb.tile([P, 1], F32, name=f"rec{h}")
             nc.vector.reciprocal(rec[:], den[:])
             y = sb.tile([P, I], F32, name=f"y{h}", align_bytes=64)
-            nc.vector.tensor_scalar(y[:], d[:], rec[:], None, ALU.mult)
+            nc.vector.tensor_scalar(y[:], na[:], shift[:], rec[:], ALU.add, ALU.mult)
             nc.sync.dma_start(out=out[P * h : P * (h + 1), :], in_=y[:])

@@ -109,7 +109,9 @@ def tile_list_meet_overtable_plain_spread_kernel(
                 stop=True,
             )
 
+        deal(nc.scalar.copy, wb_w, wb_raw, 8)
         nc.scalar.activation(tb_g[2][:], tb_rows[2][:].indirect(list_v[:]), ACT.Copy)
+        deal(nc.scalar.copy, wb_s, wbs_raw, 2)
         nc.scalar.activation(tb_g[3][:], tb_rows[3][:].indirect(list_v[:]), ACT.Copy)
 
         diff = sb.tile([P, PACK, J], BF16, name="diff", align_bytes=64)
@@ -119,8 +121,6 @@ def tile_list_meet_overtable_plain_spread_kernel(
 
         take_off(0)
         take_off(1)
-        deal(nc.gpsimd.tensor_copy, wb_w, wb_raw, 8)
-        deal(nc.gpsimd.tensor_copy, wb_s, wbs_raw, 2)
         take_off(2)
         take_off(3)
 

@@ -40,15 +40,18 @@ def tile_list_meet_overtable_plain_spread_kernel(
         list_i = sb.tile([P, I // 16], U16, name="list_i")
         x_w = sb.tile([P, T], U16, name="x_w", align_bytes=64)
         x_s = sb.tile([P, T], U8, name="x_s", align_bytes=64)
-        wa_raw = sb.tile([P, R // 2], U32, name="wa_raw", align_bytes=64)
+        wa_raw = sb.tile([P, R], U16, name="wa_raw", align_bytes=64)
         wb_raw = sb.tile([P, R], U32, name="wb_raw", align_bytes=64)
-        was_raw = sb.tile([P, R // 4], U32, name="was_raw", align_bytes=64)
-        wbs_raw = sb.tile([P, R // 4], U32, name="wbs_raw", align_bytes=64)
-        tb_rows = [sb.tile([P, V], F32, name=f"tb_rows{t}", align_bytes=64) for t in range(PACK)]
+        was_raw = sb.tile([P, R], U8, name="was_raw", align_bytes=64)
+        wbs_raw = sb.tile([P, R], U8, name="wbs_raw", tag="wbs_raw", align_bytes=64)
+        tb_01 = sb.tile([P, 2, V], F32, name="tb_01", align_bytes=64)
+        tb_2 = sb.tile([P, V], F32, name="tb_2", align_bytes=64)
+        tb_3 = sb.tile([P, V], F32, name="tb_3", align_bytes=64)
+        tb_rows = [tb_01[:, 0, :], tb_01[:, 1, :], tb_2[:], tb_3[:]]
         bi_col = sb.tile([P, 8], F32, name="bi_col")
         ident = sb.tile([P, P], F32, name="ident")
 
-        tb_view = tb.rearrange("(b t q) v -> t b q v", t=PACK, q=8)
+        tb_view = tb.rearrange("(p t) v -> p t v", t=PACK)
         nc.vector.memset(x_s[:].bitcast(I32), 0)
         nc.vector.memset(was_raw[:].bitcast(I32), 0)
         nc.vector.memset(wbs_raw[:].bitcast(I32), 0)
@@ -56,18 +59,17 @@ def tile_list_meet_overtable_plain_spread_kernel(
         nc.scalar.dma_start(out=x_w[:].bitcast(I32), in_=xt_words[0].bitcast(I32))
         load_scale_rows(nc.sync, x_s, xt_scales, (0, 1))
         load_scale_rows(nc.scalar, x_s, xt_scales, (2, 3))
-        nc.sync.dma_start(out=tb_rows[0][:], in_=tb_view[0])
-        nc.scalar.dma_start(out=tb_rows[1][:], in_=tb_view[1])
         nc.sync.dma_start(out=wa_raw[:].bitcast(I32), in_=wa_words[0].bitcast(I32))
+        nc.scalar.dma_start(out=tb_01[:], in_=tb_view[:, 0:2, :])
         nc.sync.dma_start(list_v[:], offs2)
         load_scale_rows(nc.sync, was_raw, wa_scales, range(4))
         nc.sync.dma_start(list_i[:], offs3)
         nc.sync.dma_start(out=wb_raw[:].bitcast(I32), in_=wb_words[0].rearrange("p n t -> p (n t)").bitcast(I32))
-        nc.sync.dma_start(out=tb_rows[2][:], in_=tb_view[2])
+        nc.sync.dma_start(out=tb_2[:], in_=tb_view[:, 2, :])
         load_scale_rows(nc.sync, wbs_raw, wb_scales, range(4))
-        nc.sync.dma_start(out=tb_rows[3][:], in_=tb_view[3])
+        nc.sync.dma_start(out=tb_3[:], in_=tb_view[:, 3, :])
         with nc.allow_non_contiguous_dma(reason="one bias value to a partition"):
-            nc.sync.dma_start(out=bi_col[:, 0:2], in_=bi.rearrange("o (c p) -> p (o c)", p=P))
+            nc.gpsimd.dma_start(out=bi_col[:, 0:2], in_=bi.rearrange("o (c p) -> p (o c)", p=P))
         make_identity(nc, ident[:])
 
         xa_w = sb.tile([P, J], U16, name="xa_w", align_bytes=64)
@@ -79,20 +81,20 @@ def tile_list_meet_overtable_plain_spread_kernel(
 
         def deal(engine_copy, dst, src, run):
             engine_copy(
-                dst[:].rearrange("p (t b w) -> p t b w", t=PACK, w=run),
-                src[:].rearrange("p (b t w) -> p t b w", t=PACK, w=run),
+                dst[:].rearrange("p (t c e) -> p c t e", t=PACK, e=run),
+                src[:].rearrange("p (c e t) -> p c t e", t=PACK, e=run),
             )
 
-        wa_w = sb.tile([P, R // 2], U32, name="wa_w", align_bytes=64)
-        wa_s = sb.tile([P, R // 4], U32, name="wa_s", align_bytes=64)
+        wa_w = sb.tile([P, R], U16, name="wa_w", align_bytes=64)
+        wa_s = sb.tile([P, R], U8, name="wa_s", align_bytes=64)
         wb_w = sb.tile([P, R], U32, name="wb_w", align_bytes=64)
-        wb_s = sb.tile([P, R // 4], U32, name="wb_s", align_bytes=64)
+        wb_s = sb.tile([P, R], U8, name="wb_s", align_bytes=64)
         tb_g = [sb.tile([P, J], F32, name=f"tb_g{t}", align_bytes=64) for t in range(PACK)]
 
-        deal(nc.scalar.copy, wa_w, wa_raw, 4)
-        deal(nc.vector.tensor_copy, wa_s, was_raw, 2)
-        nc.scalar.activation(tb_g[0][:], tb_rows[0][:].indirect(list_v[:]), ACT.Copy)
-        nc.scalar.activation(tb_g[1][:], tb_rows[1][:].indirect(list_v[:]), ACT.Copy)
+        deal(nc.scalar.copy, wa_w, wa_raw, 8)
+        deal(nc.vector.tensor_copy, wa_s, was_raw, 16)
+        nc.scalar.activation(tb_g[0][:], tb_rows[0].indirect(list_v[:]), ACT.Copy)
+        nc.scalar.activation(tb_g[1][:], tb_rows[1].indirect(list_v[:]), ACT.Copy)
 
         nc.vector.tensor_copy(xb_w[:], x_w[:].indirect(list_i[:]))
         nc.vector.tensor_copy(xb_s[:], x_s[:].indirect(list_i[:]))
@@ -101,20 +103,20 @@ def tile_list_meet_overtable_plain_spread_kernel(
         for t in range(PACK):
             nc.tensor.matmul_mx(
                 out=za[t // 2][:, t % 2, :],
-                lhsT=wa_w[:, 64 * t : 64 * (t + 1)].bitcast(E2M1),
-                lhsT_scale=wa_s[:, 32 * t : 32 * (t + 1)].bitcast(U8),
+                lhsT=wa_w[:, P * t : P * (t + 1)].bitcast(E2M1),
+                lhsT_scale=wa_s[:, P * t : P * (t + 1)],
                 rhs=xa_w[:].bitcast(E2M1),
                 rhs_scale=xa_s[:],
                 start=True,
                 stop=True,
             )
 
-        deal(nc.scalar.copy, wb_w, wb_raw, 8)
-        nc.scalar.activation(tb_g[2][:], tb_rows[2][:].indirect(list_v[:]), ACT.Copy)
-        deal(nc.scalar.copy, wb_s, wbs_raw, 2)
-        nc.scalar.activation(tb_g[3][:], tb_rows[3][:].indirect(list_v[:]), ACT.Copy)
+        deal(nc.scalar.copy, wb_w, wb_raw, 4)
+        nc.scalar.activation(tb_g[2][:], tb_rows[2].indirect(list_v[:]), ACT.Copy)
+        nc.scalar.activation(tb_g[3][:], tb_rows[3].indirect(list_v[:]), ACT.Copy)
 
-        diff = sb.tile([P, PACK, J], BF16, name="diff", align_bytes=64)
+        deal(nc.vector.tensor_copy, wb_s, wbs_raw, 16)
+        diff = sb.tile([P, PACK, J], BF16, name="diff", tag="wbs_raw", align_bytes=64)
 
         def take_off(t):
             nc.vector.tensor_tensor(diff[:, t, :], za[t // 2][:, t % 2, :], tb_g[t][:], ALU.subtract)
@@ -131,7 +133,7 @@ def tile_list_meet_overtable_plain_spread_kernel(
                 nc.tensor.matmul_mx(
                     out=zb[h][:, t, :],
                     lhsT=wb_w[:, P * t : P * (t + 1)].bitcast(E5M2),
-                    lhsT_scale=wb_s[:, 32 * t : 32 * (t + 1)].bitcast(U8),
+                    lhsT_scale=wb_s[:, P * t : P * (t + 1)],
                     rhs=xb_w[:, cols].bitcast(E2M1),
                     rhs_scale=xb_s[:, cols],
                     start=True,

from contextlib import ExitStack

import concourse.mybir as mybir
from concourse.masks import make_identity

K, T, J, I, R, V = 512, 512, 256, 256, 512, 512
FLOPS = 2 * K * R * (J + I) + 2 * R * J * I

F32 = mybir.dt.float32
BF16 = mybir.dt.bfloat16
I32 = mybir.dt.int32
U32 = mybir.dt.uint32
U16 = mybir.dt.uint16
U8 = mybir.dt.uint8
E2M1 = mybir.dt.float4_e2m1fn_x4
E5M2 = mybir.dt.float8_e5m2_x4
E4M3 = mybir.dt.float8_e4m3fn_x4
ALU = mybir.AluOpType
ACT = mybir.ActivationFunctionType

P = 128
PACK = 4
HALF = 128


def tile_list_meet_overtable_plain_spread_kernel(
    tc, xt_words, xt_scales, wa_words, wa_scales, tb, wb_words, wb_scales, bi, offs, offs2, offs3, out
):
    nc = tc.nc
    with ExitStack() as ctx:
        sb = ctx.enter_context(tc.tile_pool(name="sb", bufs=1))
        ps = ctx.enter_context(tc.psum_pool(name="ps", bufs=1))

        def load_scale_rows(queue, plane, scales, quadrants):
            for q in quadrants:
                queue.dma_start(out=plane[32 * q : 32 * q + 4, :].bitcast(I32), in_=scales[0, 4 * q : 4 * q + 4, :].bitcast(I32))

        list_j = sb.tile([P, J // 16], U16, name="list_j")
        list_v = sb.tile([P, J // 16], U16, name="list_v")
        list_i = sb.tile([P, I // 16], U16, name="list_i")
        x_w = sb.tile([P, T], U16, name="x_w", align_bytes=64)
        x_s = sb.tile([P, T], U8, name="x_s", align_bytes=64)
        wa_raw = sb.tile([P, R], U16, name="wa_raw", align_bytes=64)
        wb_raw = sb.tile([P, R], U32, name="wb_raw", align_bytes=64)
        was_raw = sb.tile([P, R], U8, name="was_raw", align_bytes=64)
        wbs_raw = sb.tile([P, R], U8, name="wbs_raw", tag="wbs_raw", align_bytes=64)
        tb_01 = sb.tile([P, 2, V], F32, name="tb_01", align_bytes=64)
        tb_2 = sb.tile([P, V], F32, name="tb_2", align_bytes=64)
        tb_3 = sb.tile([P, V], F32, name="tb_3", align_bytes=64)
        tb_rows = [tb_01[:, 0, :], tb_01[:, 1, :], tb_2[:], tb_3[:]]
        bi_col = sb.tile([P, 8], F32, name="bi_col")
        ident = sb.tile([P, P], F32, name="ident")

        tb_view = tb.rearrange("(p t) v -> p t v", t=PACK)
        nc.vector.memset(x_s[:].bitcast(I32), 0)
        nc.vector.memset(was_raw[:].bitcast(I32), 0)
        nc.vector.memset(wbs_raw[:].bitcast(I32), 0)
        nc.sync.dma_start(list_j[:], offs)
        nc.scalar.dma_start(out=x_w[:].bitcast(I32), in_=xt_words[0].bitcast(I32))
        load_scale_rows(nc.sync, x_s, xt_scales, (0, 1))
        load_scale_rows(nc.scalar, x_s, xt_scales, (2, 3))
        nc.sync.dma_start(out=wa_raw[:].bitcast(I32), in_=wa_words[0].bitcast(I32))
        nc.scalar.dma_start(out=tb_01[:], in_=tb_view[:, 0:2, :])
        nc.sync.dma_start(list_v[:], offs2)
        load_scale_rows(nc.sync, was_raw, wa_scales, range(4))
        nc.sync.dma_start(list_i[:], offs3)
        nc.sync.dma_start(out=wb_raw[:].bitcast(I32), in_=wb_words[0].rearrange("p n t -> p (n t)").bitcast(I32))
        nc.sync.dma_start(out=tb_2[:], in_=tb_view[:, 2, :])
        load_scale_rows(nc.sync, wbs_raw, wb_scales, range(4))
        nc.sync.dma_start(out=tb_3[:], in_=tb_view[:, 3, :])
        with nc.allow_non_contiguous_dma(reason="one bias value to a partition"):
            nc.gpsimd.dma_start(out=bi_col[:, 0:2], in_=bi.rearrange("o (c p) -> p (o c)", p=P))
        make_identity(nc, ident[:])

        xa_w = sb.tile([P, J], U16, name="xa_w", align_bytes=64)
        xa_s = sb.tile([P, J], U8, name="xa_s", align_bytes=64)
        xb_w = sb.tile([P, I], U16, name="xb_w", align_bytes=64)
        xb_s = sb.tile([P, I], U8, name="xb_s", align_bytes=64)
        nc.vector.tensor_copy(xa_w[:], x_w[:].indirect(list_j[:]))
        nc.vector.tensor_copy(xa_s[:], x_s[:].indirect(list_j[:]))

        def deal(engine_copy, dst, src, run):
            engine_copy(
                dst[:].rearrange("p (t c e) -> p c t e", t=PACK, e=run),
                src[:].rearrange("p (c e t) -> p c t e", t=PACK, e=run),
            )

        wa_w = sb.tile([P, R], U16, name="wa_w", align_bytes=64)
        wa_s = sb.tile([P, R], U8, name="wa_s", align_bytes=64)
        wb_w = sb.tile([P, R], U32, name="wb_w", align_bytes=64)
        wb_s = sb.tile([P, R], U8, name="wb_s", align_bytes=64)
        tb_g = [sb.tile([P, J], F32, name=f"tb_g{t}", align_bytes=64) for t in range(PACK)]

        deal(nc.scalar.copy, wa_w, wa_raw, 8)
        deal(nc.vector.tensor_copy, wa_s, was_raw, 16)
        nc.scalar.activation(tb_g[0][:], tb_rows[0].indirect(list_v[:]), ACT.Copy)
        nc.scalar.activation(tb_g[1][:], tb_rows[1].indirect(list_v[:]), ACT.Copy)

        nc.vector.tensor_copy(xb_w[:], x_w[:].indirect(list_i[:]))
        nc.vector.tensor_copy(xb_s[:], x_s[:].indirect(list_i[:]))

        za = [ps.tile([P, 2, J], F32, name=f"za{u}") for u in range(2)]
        for t in range(PACK):
            nc.tensor.matmul_mx(
                out=za[t // 2][:, t % 2, :],
                lhsT=wa_w[:, P * t : P * (t + 1)].bitcast(E2M1),
                lhsT_scale=wa_s[:, P * t : P * (t + 1)],
                rhs=xa_w[:].bitcast(E2M1),
                rhs_scale=xa_s[:],
                start=True,
                stop=True,
            )

        deal(nc.scalar.copy, wb_w, wb_raw, 4)
        nc.scalar.activation(tb_g[2][:], tb_rows[2].indirect(list_v[:]), ACT.Copy)
        nc.scalar.activation(tb_g[3][:], tb_rows[3].indirect(list_v[:]), ACT.Copy)

        deal(nc.vector.tensor_copy, wb_s, wbs_raw, 16)
        diff = sb.tile([P, PACK, J], BF16, name="diff", tag="wbs_raw", align_bytes=64)

        def take_off(t):
            nc.vector.tensor_tensor(diff[:, t, :], za[t // 2][:, t % 2, :], tb_g[t][:], ALU.subtract)

        take_off(0)
        take_off(1)
        take_off(2)
        take_off(3)

        zb = [ps.tile([P, PACK, HALF], F32, name=f"zb{h}", tag=f"zb{h}") for h in range(2)]
        for h in range(2):
            cols = slice(HALF * h, HALF * (h + 1))
            for t in range(PACK):
                nc.tensor.matmul_mx(
                    out=zb[h][:, t, :],
                    lhsT=wb_w[:, P * t : P * (t + 1)].bitcast(E5M2),
                    lhsT_scale=wb_s[:, P * t : P * (t + 1)],
                    rhs=xb_w[:, cols].bitcast(E2M1),
                    rhs_scale=xb_s[:, cols],
                    start=True,
                    stop=True,
                )

        hb = [sb.tile([P, HALF, PACK], BF16, name=f"hb{h}", align_bytes=64) for h in range(2)]
        ha = [sb.tile([P, HALF, PACK], BF16, name=f"ha{h}", align_bytes=64) for h in range(2)]
        hb_w = sb.tile([P, I], U32, name="hb_w", align_bytes=64)
        hb_s = sb.tile([P, I], U8, name="hb_s", align_bytes=64)
        ha_w = [sb.tile([P, HALF], U32, name=f"ha_w{h}", align_bytes=64) for h in range(2)]
        ha_s = [sb.tile([P, HALF], U8, name=f"ha_s{h}", align_bytes=64) for h in range(2)]
        for h in range(2):
            nc.scalar.activation(hb[h][:], zb[h][:].rearrange("p t i -> p i t"), ACT.Relu)
        bias_ps = ps.tile([P, I], F32, name="bias_ps", tag="zb0")
        for c in range(2):
            nc.tensor.transpose(bias_ps[:, P * c : P * (c + 1)], bi_col[:, c : c + 1].to_broadcast([P, P]), ident[:])
        nbias = sb.tile([P, I], F32, name="nbias", align_bytes=64)
        nc.scalar.activation(nbias[:], bias_ps[:], ACT.Copy, scale=-1.0 / I)

        def relu_weave(h):
            nc.vector.tensor_scalar(
                ha[h][:].rearrange("p (c e) t -> p c t e", e=4),
                diff[:, :, HALF * h : HALF * (h + 1)].rearrange("p t (c e) -> p c t e", e=4),
                0.0,
                None,
                ALU.max,
            )

        def quantize(words, scales, src, fmt):
            nc.vector.quantize_mx(out=words.bitcast(fmt), scales=scales, in_=src[:].rearrange("p c t -> p (c t)"))

        relu_weave(0)
        quantize(hb_w[:, 0:HALF], hb_s[:, 0:HALF], hb[0], E4M3)
        relu_weave(1)
        quantize(ha_w[0][:], ha_s[0][:], ha[0], E5M2)
        quantize(hb_w[:, HALF:I], hb_s[:, HALF:I], hb[1], E4M3)
        quantize(ha_w[1][:], ha_s[1][:], ha[1], E5M2)

        for h in range(2):
            a0 = ps.tile([P, I], F32, name=f"a0_{h}")
            nc.tensor.matmul_mx(
                out=a0[:],
                lhsT=ha_w[h][:].bitcast(E5M2),
                lhsT_scale=ha_s[h][:],
                rhs=hb_w[:].bitcast(E4M3),
                rhs_scale=hb_s[:],
                start=True,
                stop=True,
            )
            na = sb.tile([P, I], F32, name=f"na{h}", align_bytes=64)
            nmean = sb.tile([P, 1], F32, name=f"nmean{h}")
            nc.vector.scalar_tensor_tensor(na[:], a0[:], -1.0 / I, nbias[:], ALU.mult, ALU.add, accum_out=nmean[:])
            mag = sb.tile([P, I], F32, name=f"mag{h}", align_bytes=64)
            mag_sum = sb.tile([P, 1], F32, name=f"mag_sum{h}")
            nc.scalar.activation(mag[:], na[:], ACT.Abs, bias=nmean[:], scale=-float(I), accum_out=mag_sum[:])
            shift = sb.tile([P, 1], F32, name=f"shift{h}")
            nc.vector.tensor_scalar(shift[:], nmean[:], -1.0 / I, None, ALU.mult)
            den = sb.tile([P, 1], F32, name=f"den{h}")
            nc.vector.tensor_scalar(den[:], mag_sum[:], -1.0 / (I * I), -4.0 / I, ALU.mult, ALU.add)
            rec = sb.tile([P, 1], F32, name=f"rec{h}")
            nc.vector.reciprocal(rec[:], den[:])
            y = sb.tile([P, I], F32, name=f"y{h}", align_bytes=64)
            nc.vector.tensor_scalar(y[:], na[:], shift[:], rec[:], ALU.add, ALU.mult)
            nc.sync.dma_start(out=out[P * h : P * (h + 1), :], in_=y[:])
